import numpy as np
import ml_dtypes


def mxq(x, axis, fmt="e4m3"):
    dtype, down = {"e4m3": (ml_dtypes.float8_e4m3fn, 7), "e5m2": (ml_dtypes.float8_e5m2, 14)}[fmt]
    v = np.moveaxis(np.asarray(x, np.float32).astype(ml_dtypes.bfloat16).astype(np.float64), axis, -1)
    blocks = v.reshape(v.shape[:-1] + (-1, 32))
    amax = np.abs(blocks).max(-1, keepdims=True)
    byte = np.maximum(np.where(amax > 0, np.frexp(amax)[1] - 1 + 127, 0) - down, 1)
    scale = np.exp2(byte - 127.0)
    codes = (blocks / scale).astype(np.float32).astype(dtype).astype(np.float64)
    return np.moveaxis((codes * scale).reshape(v.shape), -1, axis)


WIDE = False


def mx_kscale(k):
    if not WIDE:
        return np.ones(k)
    levels = np.array([10, -10, 5, -5, 0])
    if k % 512:
        return np.exp2(np.random.permutation(np.resize(levels, k // 32))).repeat(32)
    a = np.empty((k // 512, 16))
    for p in range(k // 512):
        a[p, :8] = np.random.permutation(np.resize(levels, 8))
        for g in range(8):
            far = levels[np.abs(levels - a[p, g]) >= 10]
            a[p, g + 8] = far[np.random.randint(len(far))]
    return np.exp2(a.ravel()).repeat(32)


def f64(x):
    return np.asarray(x).astype(np.float64)


def striped(idx):
    return np.tile(idx.reshape(-1, 16).T, (8, 1)).astype(np.uint16)


def unstriped(offs):
    return offs[:16].T.reshape(-1).astype(np.int64)


def striped8(idx):
    return np.concatenate([x.reshape(-1, 16).T for x in idx]).astype(np.uint16)


def runs(offs, k):
    lists = np.stack([offs[16 * r : 16 * r + 16].T.reshape(-1) for r in range(8)]).astype(np.int64)
    return lists[np.arange(k) % 512 // 64]


def pack_weight(w):
    k, n = w.shape
    w = f64(np.asarray(w, np.float32).astype(ml_dtypes.bfloat16)).reshape(k // 32, 32, n)
    amax = np.abs(w).max(1)
    byte = np.clip(np.where(amax > 0, np.frexp(amax)[1] - 1 + 127 - 7, 1), 1, 254)
    scaled = (w * np.exp2(127.0 - byte)[:, None, :]).reshape(k, n).astype(np.float32)
    words = np.ascontiguousarray(scaled.reshape(k // 512, 128, 4, n).transpose(0, 1, 3, 2)).astype(ml_dtypes.float8_e4m3fn).view(np.uint8)
    return words, np.ascontiguousarray(byte.astype(np.uint8).reshape(k // 512, 16, n))


def unpack_weight(words, scales):
    g, p, n, _ = words.shape
    vals = np.ascontiguousarray(words).view(ml_dtypes.float8_e4m3fn).astype(np.float64) * np.repeat(np.exp2(scales.astype(np.float64) - 127.0), 8, axis=1)[..., None]
    return vals.transpose(0, 1, 3, 2).reshape(g * 512, n)


def sigmoid(v):
    return 1.0 / (1.0 + np.exp(-np.maximum(v, -700.0)))

def planes(y):
    n, m = y.shape
    v = y.astype(np.float32).astype(ml_dtypes.bfloat16).astype(np.float64).reshape(n // 32, 32, m)
    top = np.abs(v).max(1)
    byte = np.clip(np.where(top > 0, np.frexp(top)[1] - 1 + 127 - 7, 1), 1, 254)
    codes = (v * np.exp2(127.0 - byte)[:, None, :]).reshape(n, m).astype(np.float32).astype(ml_dtypes.float8_e4m3fn).view(np.uint8)
    words = codes.reshape(n // 512, 128, 4, m).transpose(0, 1, 3, 2)
    return np.ascontiguousarray(words), np.ascontiguousarray(byte.astype(np.uint8).reshape(n // 512, 16, m))


K, T, S, G, H = 512, 2048, 512, 2048, 512


def setup_inputs():
    n = np.random.standard_normal
    s = mx_kscale(K)[:, None]
    packed_xT = pack_weight(n((K, T)) * s)
    packed_dT = pack_weight(n((K, G)) / s)
    return {
        "x_words": packed_xT[0],
        "x_scales": packed_xT[1],
        "d_words": packed_dT[0],
        "d_scales": packed_dT[1],
        "gs": (np.random.uniform(0.5, 1.5, (K, 1)) * s).astype(np.float32),
        "offs": striped(np.random.permutation(T)[:S]),
        "k1": striped8(np.random.randint(0, G, (8, H))),
        "k2": striped8(np.random.randint(0, G, (8, H))),
        "k3": striped8(np.random.randint(0, G, (8, H))),
    }


def reference(x_words, x_scales, d_words, d_scales, gs, offs, k1, k2, k3):
    d_k3 = unpack_weight(d_words, d_scales)[np.arange(K)[:, None], runs(k3, K)]
    d_k1 = unpack_weight(d_words, d_scales)[np.arange(K)[:, None], runs(k1, K)]
    xq = unpack_weight(x_words, x_scales)[:, unstriped(offs)]
    a = 0.0625 * (d_k1.T @ xq)
    d_k2 = unpack_weight(d_words, d_scales)[np.arange(K)[:, None], runs(k2, K)]
    b = sigmoid(0.0625 * (d_k2.T @ xq))
    z = f64(gs) * (a * b)
    out_0 = 0.0625 * ((d_k3.T @ mxq(z, 0, "e4m3")))
    return (out_0,) + planes(out_0)

@@ -1,0 +1,200 @@
+from contextlib import ExitStack
+
+import concourse.mybir as mybir
+
+K, T, S, G, H = 512, 2048, 512, 2048, 512
+FLOPS = 3 * 2 * K * H * S
+
+F32 = mybir.dt.float32
+BF16 = mybir.dt.bfloat16
+I32 = mybir.dt.int32
+U32 = mybir.dt.uint32
+U16 = mybir.dt.uint16
+U8 = mybir.dt.uint8
+FP8X4 = mybir.dt.float8_e4m3fn_x4
+ACT = mybir.ActivationFunctionType
+ALU = mybir.AluOpType
+
+P = 128
+PACK = 4
+HALF = 256
+CHUNK = 128
+SIXTEENTH = 0.0625
+ROUNDED_ON_SCALAR = 2
+
+
+def tile_picked_pqglu2_sigmoid_po_kernel(
+    tc, x_words, x_scales, d_words, d_scales, gs, offs, k1, k2, k3, out_0, out_1, out_2
+):
+    nc = tc.nc
+    with ExitStack() as ctx:
+        keep = ctx.enter_context(tc.tile_pool(name="keep", bufs=1))
+        stage = ctx.enter_context(tc.tile_pool(name="stage", bufs=1))
+        psum = ctx.enter_context(tc.psum_pool(name="psum", bufs=1))
+
+        def sb(name, shape, dtype):
+            return keep.tile(shape, dtype, name=name, align_bytes=64)
+
+        def staged(name, shape, dtype, offset):
+            return stage.tile(shape, dtype, name=name, align_bytes=64, offset=offset)
+
+        lists = {}
+        for name, src in (("k2", k2), ("k1", k1), ("k3", k3), ("offs", offs)):
+            lists[name] = keep.tile([P, S // 16], U16, name="list_" + name)
+            nc.sync.dma_start(lists[name][:], src)
+        gain = sb("gain", [P, PACK], F32)
+        nc.sync.dma_start(gain[:], gs.rearrange("(p t) o -> p (t o)", t=PACK))
+
+        d_byte_table = sb("d_byte_table", [P, G], U8)
+        x_byte_table = sb("x_byte_table", [P, T], U8)
+        nc.vector.memset(d_byte_table[:].bitcast(I32), 0)
+        nc.vector.memset(x_byte_table[:].bitcast(I32), 0)
+        for e in range(2):
+            nc.sync.dma_start(d_byte_table[e:P:16, :].bitcast(I32), d_scales[0][e:16:2, :].bitcast(I32))
+        x_word_table = sb("x_word_table", [P, T], U32)
+        nc.sync.dma_start(x_word_table[:].bitcast(I32), x_words[0].rearrange("p n t -> p (n t)").bitcast(I32))
+        for q in range(4):
+            nc.sync.dma_start(x_byte_table[32 * q : 32 * q + 4, :].bitcast(I32), x_scales[0][4 * q : 4 * q + 4, :].bitcast(I32))
+        d_word_table = sb("d_word_table", [P, G], U32)
+        nc.sync.dma_start(d_word_table[:].bitcast(I32), d_words[0].rearrange("p n t -> p (n t)").bitcast(I32))
+
+        gain16 = sb("gain16", [P, PACK], F32)
+        nc.gpsimd.tensor_scalar(gain16[:], gain[:], SIXTEENTH, 0.0, ALU.mult, ALU.add)
+
+        def weight_bytes(names, offset):
+            n = len(names)
+            picked = staged("picked_bytes_" + names[0], [P, n, H], U8, offset)
+            for j, name in enumerate(names):
+                nc.vector.tensor_copy(picked[:, j, :], d_byte_table[:].indirect(lists[name][:]))
+            dealt = sb("dealt_bytes_" + names[0], [P, n, H], U8)
+            nc.vector.tensor_copy(
+                dealt[:].rearrange("p l (t m) -> p l t m", t=PACK), picked[:].rearrange("p l (m t) -> p l t m", t=PACK)
+            )
+            rows = dealt[:].rearrange("p l h -> p (l h)").bitcast(I32)
+            for e in range(2):
+                nc.scalar.dma_start(rows[2 + e : P : 32, :], rows[16 + e : P : 32, :])
+            return {name: dealt[:, j, :] for j, name in enumerate(names)}
+
+        def weight_words(name, offsets):
+            dealt = sb("dealt_words_" + name, [P, H], U32)
+            n = H // len(offsets)
+            for j, offset in enumerate(offsets):
+                picked = staged("picked_words_%s_%d" % (name, j), [P, n], U32, offset)
+                nc.vector.tensor_copy(picked[:], d_word_table[:].indirect(lists[name][:, j * n // 16 : (j + 1) * n // 16]))
+                nc.vector.tensor_copy(
+                    dealt[:].bitcast(I32).rearrange("p (t c i) -> p c t i", t=PACK, i=4)[:, j * n // 16 : (j + 1) * n // 16],
+                    picked[:].bitcast(I32).rearrange("p (c i t) -> p c t i", t=PACK, i=4),
+                )
+            return dealt
+
+        def token_words(h, offset):
+            picked = staged("token_words_%d" % h, [P, HALF], U32, offset)
+            nc.vector.tensor_copy(picked[:], x_word_table[:].indirect(lists["offs"][:, h * HALF // 16 : (h + 1) * HALF // 16]))
+            return picked
+
+        def product(banks, words, scales, rhs, rhs_scale):
+            per_bank = PACK // len(banks)
+            for t in range(PACK):
+                cols = slice(t * P, (t + 1) * P)
+                nc.tensor.matmul_mx(
+                    out=banks[t // per_bank][:, t % per_bank, :],
+                    lhsT=words[:, cols].bitcast(FP8X4),
+                    lhsT_scale=scales[:, cols],
+                    rhs=rhs.bitcast(FP8X4),
+                    rhs_scale=rhs_scale,
+                    start=True,
+                    stop=True,
+                )
+
+        def half_banks(first):
+            return [psum.tile([P, 2, HALF], F32, name="bank%d" % (first + u)) for u in range(2)]
+
+        def gate(h):
+            banks = half_banks(4 * h)
+            product(banks, words["k2"], scales["k2"], tokens[h][:], token_bytes[:, h * HALF : (h + 1) * HALF])
+            b = sb("b_%d" % h, [P, PACK, HALF], F32)
+            for u in range(2):
+                nc.scalar.activation(b[:, 2 * u : 2 * u + 2, :], banks[u][:], ACT.Sigmoid, scale=SIXTEENTH)
+            return b
+
+        def value(h):
+            banks = half_banks(4 * h + 2)
+            product(banks, words["k1"], scales["k1"], tokens[h][:], token_bytes[:, h * HALF : (h + 1) * HALF])
+            a = sb("a_%d" % h, [P, PACK, HALF], F32)
+            for t in range(PACK):
+                nc.scalar.activation(a[:, t, :], banks[t // 2][:, t % 2, :], ACT.Copy, scale=gain16[:, t : t + 1])
+            return a
+
+        scales = weight_bytes(["k2", "k1"], 3072)
+        token_bytes = sb("token_bytes", [P, S], U8)
+        nc.vector.tensor_copy(token_bytes[:], x_byte_table[:].indirect(lists["offs"][:]))
+        tokens = [token_words(0, 4096)]
+        words = {"k2": weight_words("k2", [0])}
+        b_half = [gate(0)]
+        words["k1"] = weight_words("k1", [1024])
+        a_half = [value(0)]
+        tokens.append(token_words(1, 0))
+        b_half.append(gate(1))
+        a_half.append(value(1))
+        scales.update(weight_bytes(["k3"], 1024))
+        words["k3"] = weight_words("k3", [2048, 1024])
+
+        chunks = S // CHUNK
+        z_round = [sb("z_round_%d" % c, [P, CHUNK * PACK], BF16) for c in range(chunks)]
+        z_words = [sb("z_words_%d" % c, [P, CHUNK], U32) for c in range(chunks)]
+        z_bytes = [sb("z_bytes_%d" % c, [P, CHUNK], U8) for c in range(chunks)]
+        y = [sb("y_%d" % c, [P, PACK, CHUNK], F32) for c in range(chunks)]
+        y_round = [sb("y_round_%d" % c, [P, CHUNK * PACK], BF16) for c in range(chunks)]
+        y_words = sb("y_words", [P, S], U32)
+        y_bytes = sb("y_bytes", [P, S], U8)
+        out_rows = out_0.rearrange("(p t) n -> p t n", t=PACK)
+
+        def make_z(c):
+            h, cols = c // 2, slice(c % 2 * CHUNK, (c % 2 + 1) * CHUNK)
+            nc.vector.tensor_tensor(
+                z_round[c][:].rearrange("p (c i t) -> p c t i", t=PACK, i=4),
+                a_half[h][:, :, cols].rearrange("p t (c i) -> p c t i", i=4),
+                b_half[h][:, :, cols].rearrange("p t (c i) -> p c t i", i=4),
+                ALU.mult,
+            )
+
+        def third(c):
+            nc.vector.quantize_mx(out=z_words[c][:].bitcast(FP8X4), scales=z_bytes[c][:], in_=z_round[c][:])
+            bank = psum.tile([P, PACK, CHUNK], F32, name="bank%d" % c)
+            product([bank], words["k3"], scales["k3"], z_words[c][:], z_bytes[c][:])
+            nc.scalar.activation(y[c][:], bank[:], ACT.Copy, scale=SIXTEENTH)
+            nc.sync.dma_start(out_rows[:, :, c * CHUNK : (c + 1) * CHUNK], y[c][:])
+            if c < ROUNDED_ON_SCALAR:
+                nc.scalar.activation(
+                    y_round[c][:].rearrange("p (n t) -> p n t", t=PACK),
+                    bank[:].rearrange("p t n -> p n t"),
+                    ACT.Copy,
+                    scale=SIXTEENTH,
+                )
+
+        def round_y(c):
+            if c >= ROUNDED_ON_SCALAR:
+                nc.vector.tensor_copy(
+                    y_round[c][:].rearrange("p (c i t) -> p c t i", t=PACK, i=4),
+                    y[c][:].rearrange("p t (c i) -> p c t i", i=4),
+                )
+
+        def planes(c):
+            cols = slice(c * CHUNK, (c + 1) * CHUNK)
+            nc.vector.quantize_mx(out=y_words[:, cols].bitcast(FP8X4), scales=y_bytes[:, cols], in_=y_round[c][:])
+
+        for c in range(chunks + 1):
+            if c < chunks:
+                make_z(c)
+            if c >= 1:
+                third(c - 1)
+        for c in range(chunks + 1):
+            if c < chunks:
+                round_y(c)
+            if c >= 1:
+                planes(c - 1)
+
+        nc.sync.dma_start(out_1[0].rearrange("p n t -> p (n t)").bitcast(I32), y_words[:].bitcast(I32))
+        for q in range(4):
+            engine = nc.scalar if q % 2 else nc.sync
+            engine.dma_start(out_2[0][4 * q : 4 * q + 4, :].bitcast(I32), y_bytes[32 * q : 32 * q + 4, :].bitcast(I32))

@@ -20,7 +20,7 @@ PACK = 4
 HALF = 256
 CHUNK = 128
 SIXTEENTH = 0.0625
-ROUNDED_ON_SCALAR = 2
+PICKED_WORDS_AT = {"k1": 0, "k2": 1536, "k3": 1536}
 
 
 def tile_picked_pqglu2_sigmoid_po_kernel(
@@ -39,7 +39,7 @@ def tile_picked_pqglu2_sigmoid_po_kernel(
             return stage.tile(shape, dtype, name=name, align_bytes=64, offset=offset)
 
         lists = {}
-        for name, src in (("k2", k2), ("k1", k1), ("k3", k3), ("offs", offs)):
+        for name, src in (("k1", k1), ("k2", k2), ("k3", k3), ("offs", offs)):
             lists[name] = keep.tile([P, S // 16], U16, name="list_" + name)
             nc.sync.dma_start(lists[name][:], src)
         gain = sb("gain", [P, PACK], F32)
@@ -61,29 +61,40 @@ def tile_picked_pqglu2_sigmoid_po_kernel(
         gain16 = sb("gain16", [P, PACK], F32)
         nc.gpsimd.tensor_scalar(gain16[:], gain[:], SIXTEENTH, 0.0, ALU.mult, ALU.add)
 
-        def weight_bytes(names, offset):
-            n = len(names)
-            picked = staged("picked_bytes_" + names[0], [P, n, H], U8, offset)
+        warm = sb("warm", [P, 1], F32)
+        nc.scalar.activation(warm[:], gain[:, 0:1], ACT.Sigmoid)
+
+        def pick_bytes(names, offset):
+            picked = staged("picked_bytes_" + names[0], [P, len(names), H], U8, offset)
             for j, name in enumerate(names):
                 nc.vector.tensor_copy(picked[:, j, :], d_byte_table[:].indirect(lists[name][:]))
-            dealt = sb("dealt_bytes_" + names[0], [P, n, H], U8)
-            nc.vector.tensor_copy(
-                dealt[:].rearrange("p l (t m) -> p l t m", t=PACK), picked[:].rearrange("p l (m t) -> p l t m", t=PACK)
-            )
+            return picked
+
+        def place_bytes(names, picked, queue):
+            dealt = sb("dealt_bytes_" + names[0], [P, len(names), H], U8)
+            for j in range(len(names)):
+                nc.vector.tensor_copy(
+                    dealt[:, j, :].rearrange("p (t m) -> p t m", t=PACK), picked[:, j, :].rearrange("p (m t) -> p t m", t=PACK)
+                )
             rows = dealt[:].rearrange("p l h -> p (l h)").bitcast(I32)
             for e in range(2):
-                nc.scalar.dma_start(rows[2 + e : P : 32, :], rows[16 + e : P : 32, :])
+                queue.dma_start(rows[2 + e : P : 32, :], rows[16 + e : P : 32, :])
             return {name: dealt[:, j, :] for j, name in enumerate(names)}
 
-        def weight_words(name, offsets):
-            dealt = sb("dealt_words_" + name, [P, H], U32)
-            n = H // len(offsets)
-            for j, offset in enumerate(offsets):
-                picked = staged("picked_words_%s_%d" % (name, j), [P, n], U32, offset)
-                nc.vector.tensor_copy(picked[:], d_word_table[:].indirect(lists[name][:, j * n // 16 : (j + 1) * n // 16]))
+        def pick_words(name, pieces):
+            picked = staged("picked_words_" + name, [P, H], U32, PICKED_WORDS_AT[name])
+            n = H // pieces
+            for j in range(pieces):
+                entries = lists[name][:, j * n // 16 : (j + 1) * n // 16]
+                nc.vector.tensor_copy(picked[:, j * n : (j + 1) * n], d_word_table[:].indirect(entries))
+            return picked
+
+        def deal_words(picked, dealt, pieces):
+            n = H // pieces
+            for j in range(pieces):
                 nc.vector.tensor_copy(
                     dealt[:].bitcast(I32).rearrange("p (t c i) -> p c t i", t=PACK, i=4)[:, j * n // 16 : (j + 1) * n // 16],
-                    picked[:].bitcast(I32).rearrange("p (c i t) -> p c t i", t=PACK, i=4),
+                    picked[:, j * n : (j + 1) * n].bitcast(I32).rearrange("p (c i t) -> p c t i", t=PACK, i=4),
                 )
             return dealt
 
@@ -106,45 +117,43 @@ def tile_picked_pqglu2_sigmoid_po_kernel(
                     stop=True,
                 )
 
-        def half_banks(first):
-            return [psum.tile([P, 2, HALF], F32, name="bank%d" % (first + u)) for u in range(2)]
-
-        def gate(h):
-            banks = half_banks(4 * h)
-            product(banks, words["k2"], scales["k2"], tokens[h][:], token_bytes[:, h * HALF : (h + 1) * HALF])
-            b = sb("b_%d" % h, [P, PACK, HALF], F32)
-            for u in range(2):
-                nc.scalar.activation(b[:, 2 * u : 2 * u + 2, :], banks[u][:], ACT.Sigmoid, scale=SIXTEENTH)
+        def gate(c, b):
+            h, cols = c // 2, slice(c % 2 * CHUNK, (c % 2 + 1) * CHUNK)
+            bank = psum.tile([P, PACK, CHUNK], F32, name="bank%d" % c)
+            product([bank], words["k2"], scales["k2"], tokens[h][:, cols], token_bytes[:, c * CHUNK : (c + 1) * CHUNK])
+            nc.scalar.activation(b[:], bank[:], ACT.Sigmoid, scale=SIXTEENTH)
             return b
 
         def value(h):
-            banks = half_banks(4 * h + 2)
+            banks = [psum.tile([P, 2, HALF], F32, name="bank%d" % (4 + 2 * h + u)) for u in range(2)]
             product(banks, words["k1"], scales["k1"], tokens[h][:], token_bytes[:, h * HALF : (h + 1) * HALF])
             a = sb("a_%d" % h, [P, PACK, HALF], F32)
             for t in range(PACK):
                 nc.scalar.activation(a[:, t, :], banks[t // 2][:, t % 2, :], ACT.Copy, scale=gain16[:, t : t + 1])
             return a
 
-        scales = weight_bytes(["k2", "k1"], 3072)
+        scales = place_bytes(["k1", "k2"], pick_bytes(["k1", "k2"], 3584), nc.scalar)
         token_bytes = sb("token_bytes", [P, S], U8)
         nc.vector.tensor_copy(token_bytes[:], x_byte_table[:].indirect(lists["offs"][:]))
-        tokens = [token_words(0, 4096)]
-        words = {"k2": weight_words("k2", [0])}
-        b_half = [gate(0)]
-        words["k1"] = weight_words("k1", [1024])
+        tokens = [token_words(0, 4608)]
+        words = {"k1": deal_words(pick_words("k1", 2), sb("dealt_words_k1", [P, H], U32), 2)}
         a_half = [value(0)]
         tokens.append(token_words(1, 0))
-        b_half.append(gate(1))
         a_half.append(value(1))
-        scales.update(weight_bytes(["k3"], 1024))
-        words["k3"] = weight_words("k3", [2048, 1024])
+        picked_bytes_k3 = pick_bytes(["k3"], 1024)
+        picked_k2 = pick_words("k2", 1)
+        scales.update(place_bytes(["k3"], picked_bytes_k3, nc.sync))
+        words["k2"] = deal_words(picked_k2, sb("dealt_words_k2", [P, H], U32), 1)
+        b_chunk = [gate(c, staged("b_%d" % c, [P, PACK, CHUNK], F32, 5632 + 2048 * c)) for c in range(4)]
+        picked_k3 = pick_words("k3", 1)
 
         chunks = S // CHUNK
         z_round = [sb("z_round_%d" % c, [P, CHUNK * PACK], BF16) for c in range(chunks)]
         z_words = [sb("z_words_%d" % c, [P, CHUNK], U32) for c in range(chunks)]
         z_bytes = [sb("z_bytes_%d" % c, [P, CHUNK], U8) for c in range(chunks)]
         y = [sb("y_%d" % c, [P, PACK, CHUNK], F32) for c in range(chunks)]
-        y_round = [sb("y_round_%d" % c, [P, CHUNK * PACK], BF16) for c in range(chunks)]
+        y_half = [sb("y_round_%d" % h, [P, HALF * PACK], BF16) for h in range(2)]
+        y_round = [y_half[c // 2][:, c % 2 * CHUNK * PACK : (c % 2 + 1) * CHUNK * PACK] for c in range(chunks)]
         y_words = sb("y_words", [P, S], U32)
         y_bytes = sb("y_bytes", [P, S], U8)
         out_rows = out_0.rearrange("(p t) n -> p t n", t=PACK)
@@ -152,9 +161,9 @@ def tile_picked_pqglu2_sigmoid_po_kernel(
         def make_z(c):
             h, cols = c // 2, slice(c % 2 * CHUNK, (c % 2 + 1) * CHUNK)
             nc.vector.tensor_tensor(
-                z_round[c][:].rearrange("p (c i t) -> p c t i", t=PACK, i=4),
-                a_half[h][:, :, cols].rearrange("p t (c i) -> p c t i", i=4),
-                b_half[h][:, :, cols].rearrange("p t (c i) -> p c t i", i=4),
+                z_round[c][:].rearrange("p (c i t) -> p c t i", t=PACK, i=2),
+                a_half[h][:, :, cols].rearrange("p t (c i) -> p c t i", i=2),
+                b_chunk[c][:].rearrange("p t (c i) -> p c t i", i=2),
                 ALU.mult,
             )
 
@@ -162,39 +171,40 @@ def tile_picked_pqglu2_sigmoid_po_kernel(
             nc.vector.quantize_mx(out=z_words[c][:].bitcast(FP8X4), scales=z_bytes[c][:], in_=z_round[c][:])
             bank = psum.tile([P, PACK, CHUNK], F32, name="bank%d" % c)
             product([bank], words["k3"], scales["k3"], z_words[c][:], z_bytes[c][:])
+            rounded = y_round[c].rearrange("p (n t) -> p n t", t=PACK)
+            if c == chunks - 1:
+                nc.vector.tensor_scalar(rounded, bank[:].rearrange("p t n -> p n t"), SIXTEENTH, None, ALU.mult)
             nc.scalar.activation(y[c][:], bank[:], ACT.Copy, scale=SIXTEENTH)
-            nc.sync.dma_start(out_rows[:, :, c * CHUNK : (c + 1) * CHUNK], y[c][:])
-            if c < ROUNDED_ON_SCALAR:
-                nc.scalar.activation(
-                    y_round[c][:].rearrange("p (n t) -> p n t", t=PACK),
-                    bank[:].rearrange("p t n -> p n t"),
-                    ACT.Copy,
-                    scale=SIXTEENTH,
-                )
+            engine = nc.scalar if c == chunks - 1 else nc.sync
+            engine.dma_start(out_rows[:, :, c * CHUNK : (c + 1) * CHUNK], y[c][:])
+            if c == 0:
+                nc.scalar.activation(rounded, bank[:].rearrange("p t n -> p n t"), ACT.Copy, scale=SIXTEENTH)
 
         def round_y(c):
-            if c >= ROUNDED_ON_SCALAR:
-                nc.vector.tensor_copy(
-                    y_round[c][:].rearrange("p (c i t) -> p c t i", t=PACK, i=4),
-                    y[c][:].rearrange("p t (c i) -> p c t i", i=4),
-                )
+            nc.vector.tensor_copy(
+                y_round[c].rearrange("p (c i t) -> p c t i", t=PACK, i=2),
+                y[c][:].rearrange("p t (c i) -> p c t i", i=2),
+            )
 
-        def planes(c):
-            cols = slice(c * CHUNK, (c + 1) * CHUNK)
-            nc.vector.quantize_mx(out=y_words[:, cols].bitcast(FP8X4), scales=y_bytes[:, cols], in_=y_round[c][:])
+        def planes(h):
+            cols = slice(h * HALF, (h + 1) * HALF)
+            nc.vector.quantize_mx(out=y_words[:, cols].bitcast(FP8X4), scales=y_bytes[:, cols], in_=y_half[h][:])
+            nc.sync.dma_start(out_words[:, cols], y_words[:, cols].bitcast(I32))
 
-        for c in range(chunks + 1):
-            if c < chunks:
-                make_z(c)
-            if c >= 1:
-                third(c - 1)
-        for c in range(chunks + 1):
-            if c < chunks:
-                round_y(c)
-            if c >= 1:
-                planes(c - 1)
-
-        nc.sync.dma_start(out_1[0].rearrange("p n t -> p (n t)").bitcast(I32), y_words[:].bitcast(I32))
+        out_words = out_1[0].rearrange("p n t -> p (n t)").bitcast(I32)
+        make_z(0)
+        words["k3"] = deal_words(picked_k3, staged("dealt_words_k3", [P, H], U32, 5632), 1)
+        third(0)
+        make_z(1)
+        make_z(2)
+        third(1)
+        make_z(3)
+        third(2)
+        third(3)
+        round_y(1)
+        planes(0)
+        round_y(2)
+        planes(1)
         for q in range(4):
             engine = nc.scalar if q % 2 else nc.sync
             engine.dma_start(out_2[0][4 * q : 4 * q + 4, :].bitcast(I32), y_bytes[32 * q : 32 * q + 4, :].bitcast(I32))

@@ -20,7 +20,7 @@ PACK = 4
 HALF = 256
 CHUNK = 128
 SIXTEENTH = 0.0625
-PICKED_WORDS_AT = {"k1": 0, "k2": 1536, "k3": 1536}
+PICKED_WORDS_AT = {"k1": 0, "k2": 1024, "k3": 1024}
 
 
 def tile_picked_pqglu2_sigmoid_po_kernel(
@@ -132,7 +132,7 @@ def tile_picked_pqglu2_sigmoid_po_kernel(
                 nc.scalar.activation(a[:, t, :], banks[t // 2][:, t % 2, :], ACT.Copy, scale=gain16[:, t : t + 1])
             return a
 
-        scales = place_bytes(["k1", "k2"], pick_bytes(["k1", "k2"], 3584), nc.scalar)
+        scales = place_bytes(["k1", "k2", "k3"], pick_bytes(["k1", "k2", "k3"], 3072), nc.scalar)
         token_bytes = sb("token_bytes", [P, S], U8)
         nc.vector.tensor_copy(token_bytes[:], x_byte_table[:].indirect(lists["offs"][:]))
         tokens = [token_words(0, 4608)]
@@ -140,10 +140,7 @@ def tile_picked_pqglu2_sigmoid_po_kernel(
         a_half = [value(0)]
         tokens.append(token_words(1, 0))
         a_half.append(value(1))
-        picked_bytes_k3 = pick_bytes(["k3"], 1024)
-        picked_k2 = pick_words("k2", 1)
-        scales.update(place_bytes(["k3"], picked_bytes_k3, nc.sync))
-        words["k2"] = deal_words(picked_k2, sb("dealt_words_k2", [P, H], U32), 1)
+        words["k2"] = deal_words(pick_words("k2", 2), sb("dealt_words_k2", [P, H], U32), 2)
         b_chunk = [gate(c, staged("b_%d" % c, [P, PACK, CHUNK], F32, 5632 + 2048 * c)) for c in range(4)]
         picked_k3 = pick_words("k3", 1)
 
@@ -152,7 +149,7 @@ def tile_picked_pqglu2_sigmoid_po_kernel(
         z_words = [sb("z_words_%d" % c, [P, CHUNK], U32) for c in range(chunks)]
         z_bytes = [sb("z_bytes_%d" % c, [P, CHUNK], U8) for c in range(chunks)]
         y = [sb("y_%d" % c, [P, PACK, CHUNK], F32) for c in range(chunks)]
-        y_half = [sb("y_round_%d" % h, [P, HALF * PACK], BF16) for h in range(2)]
+        y_half = [staged("y_round_0", [P, HALF * PACK], BF16, 5632 + 2048 * 3), sb("y_round_1", [P, HALF * PACK], BF16)]
         y_round = [y_half[c // 2][:, c % 2 * CHUNK * PACK : (c % 2 + 1) * CHUNK * PACK] for c in range(chunks)]
         y_words = sb("y_words", [P, S], U32)
         y_bytes = sb("y_bytes", [P, S], U8)
@@ -172,12 +169,9 @@ def tile_picked_pqglu2_sigmoid_po_kernel(
             bank = psum.tile([P, PACK, CHUNK], F32, name="bank%d" % c)
             product([bank], words["k3"], scales["k3"], z_words[c][:], z_bytes[c][:])
             rounded = y_round[c].rearrange("p (n t) -> p n t", t=PACK)
-            if c == chunks - 1:
-                nc.vector.tensor_scalar(rounded, bank[:].rearrange("p t n -> p n t"), SIXTEENTH, None, ALU.mult)
             nc.scalar.activation(y[c][:], bank[:], ACT.Copy, scale=SIXTEENTH)
-            engine = nc.scalar if c == chunks - 1 else nc.sync
-            engine.dma_start(out_rows[:, :, c * CHUNK : (c + 1) * CHUNK], y[c][:])
-            if c == 0:
+            nc.sync.dma_start(out_rows[:, :, c * CHUNK : (c + 1) * CHUNK], y[c][:])
+            if c == chunks - 1:
                 nc.scalar.activation(rounded, bank[:].rearrange("p t n -> p n t"), ACT.Copy, scale=SIXTEENTH)
 
         def round_y(c):
@@ -189,7 +183,6 @@ def tile_picked_pqglu2_sigmoid_po_kernel(
         def planes(h):
             cols = slice(h * HALF, (h + 1) * HALF)
             nc.vector.quantize_mx(out=y_words[:, cols].bitcast(FP8X4), scales=y_bytes[:, cols], in_=y_half[h][:])
-            nc.sync.dma_start(out_words[:, cols], y_words[:, cols].bitcast(I32))
 
         out_words = out_1[0].rearrange("p n t -> p (n t)").bitcast(I32)
         make_z(0)
@@ -201,10 +194,12 @@ def tile_picked_pqglu2_sigmoid_po_kernel(
         make_z(3)
         third(2)
         third(3)
+        round_y(0)
         round_y(1)
-        planes(0)
         round_y(2)
+        planes(0)
         planes(1)
+        nc.sync.dma_start(out_words, y_words[:].bitcast(I32))
         for q in range(4):
             engine = nc.scalar if q % 2 else nc.sync
             engine.dma_start(out_2[0][4 * q : 4 * q + 4, :].bitcast(I32), y_bytes[32 * q : 32 * q + 4, :].bitcast(I32))

@@ -119,9 +119,10 @@ def tile_picked_pqglu2_sigmoid_po_kernel(
 
         def gate(c, b):
             h, cols = c // 2, slice(c % 2 * CHUNK, (c % 2 + 1) * CHUNK)
-            bank = psum.tile([P, PACK, CHUNK], F32, name="bank%d" % c)
-            product([bank], words["k2"], scales["k2"], tokens[h][:, cols], token_bytes[:, c * CHUNK : (c + 1) * CHUNK])
-            nc.scalar.activation(b[:], bank[:], ACT.Sigmoid, scale=SIXTEENTH)
+            banks = [psum.tile([P, 2, CHUNK], F32, name="bank%d" % (2 * c + u)) for u in range(2)]
+            product(banks, words["k2"], scales["k2"], tokens[h][:, cols], token_bytes[:, c * CHUNK : (c + 1) * CHUNK])
+            for u in range(2):
+                nc.scalar.activation(b[:, 2 * u : 2 * u + 2, :], banks[u][:], ACT.Sigmoid, scale=SIXTEENTH)
             return b
 
         def value(h):
@@ -166,13 +167,11 @@ def tile_picked_pqglu2_sigmoid_po_kernel(
 
         def third(c):
             nc.vector.quantize_mx(out=z_words[c][:].bitcast(FP8X4), scales=z_bytes[c][:], in_=z_round[c][:])
-            bank = psum.tile([P, PACK, CHUNK], F32, name="bank%d" % c)
-            product([bank], words["k3"], scales["k3"], z_words[c][:], z_bytes[c][:])
-            rounded = y_round[c].rearrange("p (n t) -> p n t", t=PACK)
-            nc.scalar.activation(y[c][:], bank[:], ACT.Copy, scale=SIXTEENTH)
+            banks = [psum.tile([P, 2, CHUNK], F32, name="bank%d" % (2 * c + u)) for u in range(2)]
+            product(banks, words["k3"], scales["k3"], z_words[c][:], z_bytes[c][:])
+            for u in range(2):
+                nc.scalar.activation(y[c][:, 2 * u : 2 * u + 2, :], banks[u][:], ACT.Copy, scale=SIXTEENTH)
             nc.sync.dma_start(out_rows[:, :, c * CHUNK : (c + 1) * CHUNK], y[c][:])
-            if c == chunks - 1:
-                nc.scalar.activation(rounded, bank[:].rearrange("p t n -> p n t"), ACT.Copy, scale=SIXTEENTH)
 
         def round_y(c):
             nc.vector.tensor_copy(
@@ -196,8 +195,9 @@ def tile_picked_pqglu2_sigmoid_po_kernel(
         third(3)
         round_y(0)
         round_y(1)
-        round_y(2)
         planes(0)
+        round_y(2)
+        round_y(3)
         planes(1)
         nc.sync.dma_start(out_words, y_words[:].bitcast(I32))
         for q in range(4):

from contextlib import ExitStack

import concourse.mybir as mybir

K, T, S, G, H = 512, 2048, 512, 2048, 512
FLOPS = 3 * 2 * K * H * S

F32 = mybir.dt.float32
BF16 = mybir.dt.bfloat16
I32 = mybir.dt.int32
U32 = mybir.dt.uint32
U16 = mybir.dt.uint16
U8 = mybir.dt.uint8
FP8X4 = mybir.dt.float8_e4m3fn_x4
ACT = mybir.ActivationFunctionType
ALU = mybir.AluOpType

P = 128
PACK = 4
HALF = 256
CHUNK = 128
SIXTEENTH = 0.0625
PICKED_WORDS_AT = {"k1": 0, "k2": 1024, "k3": 1024}


def tile_picked_pqglu2_sigmoid_po_kernel(
    tc, x_words, x_scales, d_words, d_scales, gs, offs, k1, k2, k3, out_0, out_1, out_2
):
    nc = tc.nc
    with ExitStack() as ctx:
        keep = ctx.enter_context(tc.tile_pool(name="keep", bufs=1))
        stage = ctx.enter_context(tc.tile_pool(name="stage", bufs=1))
        psum = ctx.enter_context(tc.psum_pool(name="psum", bufs=1))

        def sb(name, shape, dtype):
            return keep.tile(shape, dtype, name=name, align_bytes=64)

        def staged(name, shape, dtype, offset):
            return stage.tile(shape, dtype, name=name, align_bytes=64, offset=offset)

        lists = {}
        for name, src in (("k1", k1), ("k2", k2), ("k3", k3), ("offs", offs)):
            lists[name] = keep.tile([P, S // 16], U16, name="list_" + name)
            nc.sync.dma_start(lists[name][:], src)
        gain = sb("gain", [P, PACK], F32)
        nc.sync.dma_start(gain[:], gs.rearrange("(p t) o -> p (t o)", t=PACK))

        d_byte_table = sb("d_byte_table", [P, G], U8)
        x_byte_table = sb("x_byte_table", [P, T], U8)
        nc.vector.memset(d_byte_table[:].bitcast(I32), 0)
        nc.vector.memset(x_byte_table[:].bitcast(I32), 0)
        for e in range(2):
            nc.sync.dma_start(d_byte_table[e:P:16, :].bitcast(I32), d_scales[0][e:16:2, :].bitcast(I32))
        x_word_table = sb("x_word_table", [P, T], U32)
        nc.sync.dma_start(x_word_table[:].bitcast(I32), x_words[0].rearrange("p n t -> p (n t)").bitcast(I32))
        for q in range(4):
            nc.sync.dma_start(x_byte_table[32 * q : 32 * q + 4, :].bitcast(I32), x_scales[0][4 * q : 4 * q + 4, :].bitcast(I32))
        d_word_table = sb("d_word_table", [P, G], U32)
        nc.sync.dma_start(d_word_table[:].bitcast(I32), d_words[0].rearrange("p n t -> p (n t)").bitcast(I32))

        gain16 = sb("gain16", [P, PACK], F32)
        nc.gpsimd.tensor_scalar(gain16[:], gain[:], SIXTEENTH, 0.0, ALU.mult, ALU.add)

        warm = sb("warm", [P, 1], F32)
        nc.scalar.activation(warm[:], gain[:, 0:1], ACT.Sigmoid)

        def pick_bytes(names, offset):
            picked = staged("picked_bytes_" + names[0], [P, len(names), H], U8, offset)
            for j, name in enumerate(names):
                nc.vector.tensor_copy(picked[:, j, :], d_byte_table[:].indirect(lists[name][:]))
            return picked

        def place_bytes(names, picked, queue):
            dealt = sb("dealt_bytes_" + names[0], [P, len(names), H], U8)
            for j in range(len(names)):
                nc.vector.tensor_copy(
                    dealt[:, j, :].rearrange("p (t m) -> p t m", t=PACK), picked[:, j, :].rearrange("p (m t) -> p t m", t=PACK)
                )
            rows = dealt[:].rearrange("p l h -> p (l h)").bitcast(I32)
            for e in range(2):
                queue.dma_start(rows[2 + e : P : 32, :], rows[16 + e : P : 32, :])
            return {name: dealt[:, j, :] for j, name in enumerate(names)}

        def pick_words(name, pieces):
            picked = staged("picked_words_" + name, [P, H], U32, PICKED_WORDS_AT[name])
            n = H // pieces
            for j in range(pieces):
                entries = lists[name][:, j * n // 16 : (j + 1) * n // 16]
                nc.vector.tensor_copy(picked[:, j * n : (j + 1) * n], d_word_table[:].indirect(entries))
            return picked

        def deal_words(picked, dealt, pieces):
            n = H // pieces
            for j in range(pieces):
                nc.vector.tensor_copy(
                    dealt[:].bitcast(I32).rearrange("p (t c i) -> p c t i", t=PACK, i=4)[:, j * n // 16 : (j + 1) * n // 16],
                    picked[:, j * n : (j + 1) * n].bitcast(I32).rearrange("p (c i t) -> p c t i", t=PACK, i=4),
                )
            return dealt

        def token_words(h, offset):
            picked = staged("token_words_%d" % h, [P, HALF], U32, offset)
            nc.vector.tensor_copy(picked[:], x_word_table[:].indirect(lists["offs"][:, h * HALF // 16 : (h + 1) * HALF // 16]))
            return picked

        def product(banks, words, scales, rhs, rhs_scale):
            per_bank = PACK // len(banks)
            for t in range(PACK):
                cols = slice(t * P, (t + 1) * P)
                nc.tensor.matmul_mx(
                    out=banks[t // per_bank][:, t % per_bank, :],
                    lhsT=words[:, cols].bitcast(FP8X4),
                    lhsT_scale=scales[:, cols],
                    rhs=rhs.bitcast(FP8X4),
                    rhs_scale=rhs_scale,
                    start=True,
                    stop=True,
                )

        def gate(c, b):
            h, cols = c // 2, slice(c % 2 * CHUNK, (c % 2 + 1) * CHUNK)
            banks = [psum.tile([P, 2, CHUNK], F32, name="bank%d" % (2 * c + u)) for u in range(2)]
            product(banks, words["k2"], scales["k2"], tokens[h][:, cols], token_bytes[:, c * CHUNK : (c + 1) * CHUNK])
            for u in range(2):
                nc.scalar.activation(b[:, 2 * u : 2 * u + 2, :], banks[u][:], ACT.Sigmoid, scale=SIXTEENTH)
            return b

        def value(h):
            banks = [psum.tile([P, 2, HALF], F32, name="bank%d" % (4 + 2 * h + u)) for u in range(2)]
            product(banks, words["k1"], scales["k1"], tokens[h][:], token_bytes[:, h * HALF : (h + 1) * HALF])
            a = sb("a_%d" % h, [P, PACK, HALF], F32)
            for t in range(PACK):
                nc.scalar.activation(a[:, t, :], banks[t // 2][:, t % 2, :], ACT.Copy, scale=gain16[:, t : t + 1])
            return a

        scales = place_bytes(["k1", "k2", "k3"], pick_bytes(["k1", "k2", "k3"], 3072), nc.scalar)
        token_bytes = sb("token_bytes", [P, S], U8)
        nc.vector.tensor_copy(token_bytes[:], x_byte_table[:].indirect(lists["offs"][:]))
        tokens = [token_words(0, 4608)]
        words = {"k1": deal_words(pick_words("k1", 2), sb("dealt_words_k1", [P, H], U32), 2)}
        a_half = [value(0)]
        tokens.append(token_words(1, 0))
        a_half.append(value(1))
        words["k2"] = deal_words(pick_words("k2", 2), sb("dealt_words_k2", [P, H], U32), 2)
        b_chunk = [gate(c, staged("b_%d" % c, [P, PACK, CHUNK], F32, 5632 + 2048 * c)) for c in range(4)]
        picked_k3 = pick_words("k3", 1)

        chunks = S // CHUNK
        z_round = [sb("z_round_%d" % c, [P, CHUNK * PACK], BF16) for c in range(chunks)]
        z_words = [sb("z_words_%d" % c, [P, CHUNK], U32) for c in range(chunks)]
        z_bytes = [sb("z_bytes_%d" % c, [P, CHUNK], U8) for c in range(chunks)]
        y = [sb("y_%d" % c, [P, PACK, CHUNK], F32) for c in range(chunks)]
        y_half = [staged("y_round_0", [P, HALF * PACK], BF16, 5632 + 2048 * 3), sb("y_round_1", [P, HALF * PACK], BF16)]
        y_round = [y_half[c // 2][:, c % 2 * CHUNK * PACK : (c % 2 + 1) * CHUNK * PACK] for c in range(chunks)]
        y_words = sb("y_words", [P, S], U32)
        y_bytes = sb("y_bytes", [P, S], U8)
        out_rows = out_0.rearrange("(p t) n -> p t n", t=PACK)

        def make_z(c):
            h, cols = c // 2, slice(c % 2 * CHUNK, (c % 2 + 1) * CHUNK)
            nc.vector.tensor_tensor(
                z_round[c][:].rearrange("p (c i t) -> p c t i", t=PACK, i=2),
                a_half[h][:, :, cols].rearrange("p t (c i) -> p c t i", i=2),
                b_chunk[c][:].rearrange("p t (c i) -> p c t i", i=2),
                ALU.mult,
            )

        def third(c):
            nc.vector.quantize_mx(out=z_words[c][:].bitcast(FP8X4), scales=z_bytes[c][:], in_=z_round[c][:])
            banks = [psum.tile([P, 2, CHUNK], F32, name="bank%d" % (2 * c + u)) for u in range(2)]
            product(banks, words["k3"], scales["k3"], z_words[c][:], z_bytes[c][:])
            for u in range(2):
                nc.scalar.activation(y[c][:, 2 * u : 2 * u + 2, :], banks[u][:], ACT.Copy, scale=SIXTEENTH)
            nc.sync.dma_start(out_rows[:, :, c * CHUNK : (c + 1) * CHUNK], y[c][:])

        def round_y(c):
            nc.vector.tensor_copy(
                y_round[c].rearrange("p (c i t) -> p c t i", t=PACK, i=2),
                y[c][:].rearrange("p t (c i) -> p c t i", i=2),
            )

        def planes(h):
            cols = slice(h * HALF, (h + 1) * HALF)
            nc.vector.quantize_mx(out=y_words[:, cols].bitcast(FP8X4), scales=y_bytes[:, cols], in_=y_half[h][:])

        out_words = out_1[0].rearrange("p n t -> p (n t)").bitcast(I32)
        make_z(0)
        words["k3"] = deal_words(picked_k3, staged("dealt_words_k3", [P, H], U32, 5632), 1)
        third(0)
        make_z(1)
        make_z(2)
        third(1)
        make_z(3)
        third(2)
        third(3)
        round_y(0)
        round_y(1)
        planes(0)
        round_y(2)
        round_y(3)
        planes(1)
        nc.sync.dma_start(out_words, y_words[:].bitcast(I32))
        for q in range(4):
            engine = nc.scalar if q % 2 else nc.sync
            engine.dma_start(out_2[0][4 * q : 4 * q + 4, :].bitcast(I32), y_bytes[32 * q : 32 * q + 4, :].bitcast(I32))
